import numpy as np
import ml_dtypes


def mxq(x, axis, fmt="e4m3"):
    dtype, down = {"e4m3": (ml_dtypes.float8_e4m3fn, 7), "e5m2": (ml_dtypes.float8_e5m2, 14)}[fmt]
    v = np.moveaxis(np.asarray(x, np.float32).astype(ml_dtypes.bfloat16).astype(np.float64), axis, -1)
    blocks = v.reshape(v.shape[:-1] + (-1, 32))
    amax = np.abs(blocks).max(-1, keepdims=True)
    byte = np.maximum(np.where(amax > 0, np.frexp(amax)[1] - 1 + 127, 0) - down, 1)
    scale = np.exp2(byte - 127.0)
    codes = (blocks / scale).astype(np.float32).astype(dtype).astype(np.float64)
    return np.moveaxis((codes * scale).reshape(v.shape), -1, axis)


WIDE = False


def mx_kscale(k):
    if not WIDE:
        return np.ones(k)
    levels = np.array([10, -10, 5, -5, 0])
    if k % 512:
        return np.exp2(np.random.permutation(np.resize(levels, k // 32))).repeat(32)
    a = np.empty((k // 512, 16))
    for p in range(k // 512):
        a[p, :8] = np.random.permutation(np.resize(levels, 8))
        for g in range(8):
            far = levels[np.abs(levels - a[p, g]) >= 10]
            a[p, g + 8] = far[np.random.randint(len(far))]
    return np.exp2(a.ravel()).repeat(32)


def f64(x):
    return np.asarray(x).astype(np.float64)


def striped(idx):
    return np.tile(idx.reshape(-1, 16).T, (8, 1)).astype(np.uint16)


def unstriped(offs):
    return offs[:16].T.reshape(-1).astype(np.int64)


E2M1 = np.array([0.0, 0.5, 1.0, 1.5, 2.0, 3.0, 4.0, 6.0, -0.0, -0.5, -1.0, -1.5, -2.0, -3.0, -4.0, -6.0])


def pack_weight(w, fmt):
    k, n = w.shape
    w = f64(np.asarray(w, np.float32).astype(ml_dtypes.bfloat16)).reshape(k // 32, 32, n)
    amax = np.abs(w).max(1)
    if fmt == "e4m3":
        byte = np.frexp(amax)[1] - 1 + 127 - 7
    else:
        mant, ex = np.frexp(amax / 6.0)
        byte = np.where(mant > 0.5, ex, ex - 1) + 127
    byte = np.clip(np.where(amax > 0, byte, 1), 1, 254)
    scaled = (w * np.exp2(127.0 - byte)[:, None, :]).reshape(k, n).astype(np.float32)
    by_word = np.ascontiguousarray(scaled.reshape(k // 512, 128, 4, n).transpose(0, 1, 3, 2))
    if fmt == "e4m3":
        words = by_word.astype(ml_dtypes.float8_e4m3fn).view(np.uint8)
    else:
        c = by_word.astype(ml_dtypes.float4_e2m1fn).view(np.uint8) & 0xF
        words = (c[..., 0::2] | (c[..., 1::2] << 4)).reshape(k // 512, 128, 2 * n)
    return np.ascontiguousarray(words), np.ascontiguousarray(byte.astype(np.uint8).reshape(k // 512, 16, n))


def unpack_weight(words, scales, fmt):
    g, _, n = scales.shape
    words = np.ascontiguousarray(words).reshape(g, 128, n, -1)
    if fmt == "e4m3":
        vals = words.view(ml_dtypes.float8_e4m3fn).astype(np.float64)
    else:
        nib = np.empty((g, 128, n, 4), np.uint8)
        nib[..., 0::2] = words & 0xF
        nib[..., 1::2] = words >> 4
        vals = E2M1[nib]
    vals = vals * np.repeat(np.exp2(scales.astype(np.float64) - 127.0), 8, axis=1)[..., None]
    return vals.transpose(0, 1, 3, 2).reshape(g * 512, n)


def gelu(v):
    return 0.5 * v * (1.0 + np.tanh(np.sqrt(2.0 / np.pi) * (v + 0.044715 * v**3)))


K, KA, KB, H, T, S, T3, S2 = 1536, 512, 1024, 1024, 2048, 512, 2048, 512

def setup_inputs():
    n = np.random.standard_normal
    s = mx_kscale(K)[:, None]
    u = mx_kscale(H)[:, None]
    tab_words, tab_scales = pack_weight(n((K, T)) * s, "e4m3")
    tab2_words, tab2_scales = pack_weight(n((H, T3)) / np.sqrt(H) / u, "e4m3")
    tab3_words, tab3_scales = pack_weight(n((H, T3)) / np.sqrt(H) / u, "e4m3")
    w4_words, w4_scales = pack_weight(0.56 * n((KB, H)) / np.sqrt(K) / s[KA:], "e2m1")
    return {
        "tab_words": tab_words, "tab_scales": tab_scales,
        "offs": striped(np.random.permutation(T)[:S]),
        "w1": (0.56 * n((KA, H)) / np.sqrt(K) / s[:KA]).astype(np.float32),
        "w4_words": w4_words, "w4_scales": w4_scales,
        "gain": (2.5 * np.exp(0.3 * n(H)) * u[:, 0]).astype(np.float32),
        "tab2_words": tab2_words, "tab2_scales": tab2_scales,
        "offs2": striped(np.random.permutation(T3)[:S2]),
        "tab3_words": tab3_words, "tab3_scales": tab3_scales,
        "offs3": striped(np.random.permutation(T3)[:S2]),
        "d": (0.7 * n(S2)).astype(np.float32),
    }

def reference(tab_words, tab_scales, offs, w1, w4_words, w4_scales, gain,
              tab2_words, tab2_scales, offs2, tab3_words, tab3_scales, offs3, d):
    v = unpack_weight(tab_words, tab_scales, "e4m3")[:, unstriped(offs)]
    v2 = unpack_weight(tab2_words, tab2_scales, "e4m3")[:, unstriped(offs2)]
    v3 = unpack_weight(tab3_words, tab3_scales, "e4m3")[:, unstriped(offs3)]
    w4 = unpack_weight(w4_words, w4_scales, "e2m1")
    a = mxq(f64(w1), 0, "e4m3").T @ v[:KA] + w4.T @ v[KA:]
    h = f64(gain)[:, None] * (a * np.cos(a))
    hq = mxq(h, 0, "e4m3")
    e2 = v2.T @ hq
    e3 = v3.T @ hq
    return (e2 + f64(d)[:, None]) / (1.0 + np.square(e3))

@@ -1,0 +1,258 @@
+import math
+from contextlib import ExitStack
+
+import concourse.mybir as mybir
+
+K, KA, KB, H, T, S = 1536, 512, 1024, 1024, 2048, 512
+FLOPS = 2 * K * H * S + 2 * 2 * H * S * S
+
+F32 = mybir.dt.float32
+BF16 = mybir.dt.bfloat16
+I32 = mybir.dt.int32
+U32 = mybir.dt.uint32
+U16 = mybir.dt.uint16
+U8 = mybir.dt.uint8
+FP8X4 = mybir.dt.float8_e4m3fn_x4
+FP4X4 = mybir.dt.float4_e2m1fn_x4
+ALU = mybir.AluOpType
+ACT = mybir.ActivationFunctionType
+
+P = 128
+PACK = 4
+KP = P * PACK
+
+
+def tile_list_heart_offer_score_kernel(
+    tc, tab_words, tab_scales, offs, w1, w4_words, w4_scales, gain,
+    tab2_words, tab2_scales, offs2, tab3_words, tab3_scales, offs3, d, out,
+):
+    nc = tc.nc
+    with ExitStack() as ctx:
+        keep = ctx.enter_context(tc.tile_pool(name="keep", bufs=1))
+        work = ctx.enter_context(tc.tile_pool(name="work", bufs=3))
+        psum = ctx.enter_context(tc.psum_pool(name="psum", bufs=1))
+
+        def kept(name, shape, dtype):
+            return keep.tile(shape, dtype, name=name, align_bytes=64)
+
+        def load_list(name, src):
+            tile = keep.tile([P, S // 16], U16, name=name)
+            nc.sync.dma_start(tile[:], src)
+            return tile
+
+        def load_words(name, src):
+            tile = kept(name, [P, T], I32)
+            nc.sync.dma_start(tile[:], src.rearrange("p t i -> p (t i)").bitcast(I32))
+            return tile
+
+        def gather_words(name, window, lst):
+            tile = kept(name, [P, S], U32)
+            nc.vector.tensor_copy(tile[:], window[:].bitcast(U32).indirect(lst[:]))
+            return tile
+
+        def gather_bytes(name, window, lst):
+            tile = kept(name, [P, S], U8)
+            nc.vector.tensor_copy(tile[:], window.indirect(lst[:]))
+            return tile
+
+        def load_w1(b):
+            tile = kept(f"w1_raw{b}", [P, PACK, KP], F32)
+            nc.sync.dma_start(tile[:], w1[:, b * KP:(b + 1) * KP].rearrange("(p j) c -> p j c", j=PACK))
+            return tile
+
+        def cast_w1(b, raw):
+            grouped = kept(f"w1_bf{b}", [P, KP * PACK], BF16)
+            nc.scalar.copy(
+                out=grouped[:].rearrange("p (t m j) -> p m j t", t=PACK, j=PACK),
+                in_=raw[:].rearrange("p j (m t) -> p m j t", t=PACK),
+            )
+            return grouped
+
+        def quantize(name, grouped):
+            codes = kept(name + "_codes", [P, KP], U32)
+            plane = kept(name + "_plane", [P, KP], U8)
+            nc.vector.quantize_mx(out=codes[:].bitcast(FP8X4), scales=plane[:], in_=grouped[:])
+            return codes, plane
+
+        tab_sc = kept("tab_sc", [P, 2, T], U8)
+        w4_sc_raw = kept("w4_sc_raw", [P, 2, H], U8)
+        tab3_sc = kept("tab3_sc", [P, T], U8)
+        tab2_sc = kept("tab2_sc", [P, T], U8)
+        nc.vector.memset(w4_sc_raw[:].bitcast(I32), 0)
+        nc.vector.memset(tab_sc[:].bitcast(I32), 0)
+        nc.gpsimd.memset(tab3_sc[:].bitcast(I32), 0)
+        nc.gpsimd.memset(tab2_sc[:].bitcast(I32), 0)
+
+        gain_sb = keep.tile([P, 2, PACK], F32, name="gain_sb")
+        nc.gpsimd.dma_start(gain_sb[:], gain.rearrange("(b p t) -> p b t", b=2, t=PACK))
+        d_sb = keep.tile([P, 4], F32, name="d_sb")
+        with nc.allow_non_contiguous_dma(reason="one offset a partition"):
+            nc.gpsimd.dma_start(d_sb[:], d.rearrange("(m p) -> p m", p=P))
+
+        w4_raw = kept("w4_raw", [P, 2, H], U16)
+        nc.sync.dma_start(w4_raw[:].bitcast(I32), w4_words.rearrange("a p n -> p a n").bitcast(I32))
+        lst1 = load_list("lst1", offs)
+        for q in range(4):
+            nc.sync.dma_start(
+                w4_sc_raw[32 * q:32 * q + 4, :, :].bitcast(I32),
+                w4_scales[:, 4 * q:4 * q + 4, :].rearrange("a r n -> r a n").bitcast(I32),
+            )
+        for q in range(4):
+            nc.sync.dma_start(
+                tab_sc[32 * q:32 * q + 4, :, :].bitcast(I32),
+                tab_scales[1:3, 4 * q:4 * q + 4, :].rearrange("a r n -> r a n").bitcast(I32),
+            )
+        for q in range(4):
+            nc.sync.dma_start(
+                tab_sc[32 * q + 4:32 * q + 8, 0, :].bitcast(I32),
+                tab_scales[0, 4 * q:4 * q + 4, :].bitcast(I32),
+            )
+        win1 = load_words("win1", tab_words[1])
+        w1_raw0 = load_w1(0)
+        win2 = load_words("win2", tab_words[2])
+        win0 = load_words("win0", tab_words[0])
+        w1_raw1 = load_w1(1)
+        lst3 = load_list("lst3", offs3)
+        lst2 = load_list("lst2", offs2)
+
+        def load_packed_scales(tile, src):
+            for q in range(4):
+                nc.sync.dma_start(tile[32 * q:32 * q + 8, :].bitcast(I32), src[:, 4 * q:4 * q + 4, :].bitcast(I32))
+
+        load_packed_scales(tab3_sc, tab3_scales)
+        win3 = [load_words(f"win3_{a}", tab3_words[a]) for a in range(2)]
+        load_packed_scales(tab2_sc, tab2_scales)
+        win2s = [load_words(f"win2s_{a}", tab2_words[a]) for a in range(2)]
+
+        w4_codes = []
+        w4_plane = []
+        for b in range(2):
+            codes = kept(f"w4_codes{b}", [P, 2, KP], U16)
+            nc.vector.tensor_copy(
+                out=codes[:].rearrange("p a (t m) -> p a t m", t=PACK),
+                in_=w4_raw[:, :, b * KP:(b + 1) * KP].rearrange("p a (m t) -> p a t m", t=PACK),
+            )
+            plane = kept(f"w4_plane{b}", [P, 2, KP], U8)
+            nc.vector.tensor_copy(
+                out=plane[:].rearrange("p a (t m) -> p a t m", t=PACK),
+                in_=w4_sc_raw[:, :, b * KP:(b + 1) * KP].rearrange("p a (m t) -> p a t m", t=PACK),
+            )
+            w4_codes.append(codes)
+            w4_plane.append(plane)
+
+        v_sc10 = gather_bytes("v_sc10", tab_sc[:, 0, :], lst1)
+        v_sc2 = gather_bytes("v_sc2", tab_sc[:, 1, :], lst1)
+        v1 = gather_words("v1", win1, lst1)
+        w1_bf0 = cast_w1(0, w1_raw0)
+        v2 = gather_words("v2", win2, lst1)
+        w1q = [quantize("w1q0", w1_bf0)]
+        v0 = gather_words("v0", win0, lst1)
+        w1_bf1 = cast_w1(1, w1_raw1)
+
+        banks = [psum.tile([P, S], F32, name=f"acc{i}", tag=f"bank{i}") for i in range(8)]
+
+        def w4_pass(b, t, a, words, plane):
+            cols = slice(t * P, (t + 1) * P)
+            nc.tensor.matmul_mx(
+                out=banks[4 * b + t][:], lhsT=w4_codes[b][:, a, cols].bitcast(FP4X4), lhsT_scale=w4_plane[b][:, a, cols],
+                rhs=words[:].bitcast(FP8X4), rhs_scale=plane[:], start=(a == 0), stop=False,
+            )
+
+        def w1_pass(b, t):
+            cols = slice(t * P, (t + 1) * P)
+            codes, plane = w1q[b]
+            nc.tensor.matmul_mx(
+                out=banks[4 * b + t][:], lhsT=codes[:, cols].bitcast(FP8X4), lhsT_scale=plane[:, cols],
+                rhs=v0[:].bitcast(FP8X4), rhs_scale=v_sc10[4:P, :], start=False, stop=True,
+            )
+
+        for a, words, plane in ((0, v1, v_sc10), (1, v2, v_sc2)):
+            for b in range(2):
+                for t in range(PACK):
+                    w4_pass(b, t, a, words, plane)
+        for t in range(PACK):
+            w1_pass(0, t)
+
+        h_rows = [kept(f"h_rows{b}", [P, PACK, S], BF16) for b in range(2)]
+        cosines = {}
+
+        def reduce_angle(i):
+            turns = work.tile([P, S], I32, name="turns")
+            nc.vector.tensor_scalar(turns[:], banks[i][:], 1.0 / (2.0 * math.pi), 0.25, ALU.mult, ALU.add)
+            return turns
+
+        def cosine(i, turns):
+            rest = work.tile([P, S], F32, name="rest")
+            nc.vector.scalar_tensor_tensor(rest[:], turns[:], -2.0 * math.pi, banks[i][:], ALU.mult, ALU.add)
+            cos = work.tile([P, S], F32, name="cos")
+            nc.scalar.activation(cos[:], rest[:], ACT.Sin, bias=0.5 * math.pi)
+            cosines[i] = cos
+
+        def product(i):
+            b, t = divmod(i, PACK)
+            nc.vector.scalar_tensor_tensor(
+                h_rows[b][:, t, :], banks[i][:], gain_sb[:, b, t:t + 1], cosines[i][:], ALU.mult, ALU.mult)
+
+        def weave(b, dst, eng, j0, j1):
+            eng(
+                out=dst[:, j0 * PACK:j1 * PACK].rearrange("p (c i t) -> p c t i", i=4, t=PACK),
+                in_=h_rows[b][:, :, j0:j1].rearrange("p t (c i) -> p c t i", i=4),
+            )
+
+        h_bf = [kept(f"h_bf{b}", [P, S * PACK], BF16) for b in range(2)]
+        hq = []
+        g3 = []
+        turns = {0: reduce_angle(0)}
+        for i in range(8):
+            if i + 1 < 8:
+                turns[i + 1] = reduce_angle(i + 1)
+            cosine(i, turns[i])
+            if i == 1:
+                w1q.append(quantize("w1q1", w1_bf1))
+                for t in range(PACK):
+                    w1_pass(1, t)
+            if i >= 1:
+                product(i - 1)
+            if i == 4:
+                weave(0, h_bf[0], nc.scalar.copy, 0, S)
+                g3_sc = gather_bytes("g3_sc", tab3_sc[:], lst3)
+            if i == 5:
+                g3.append(gather_words("g3_0", win3[0], lst3))
+            if i == 6:
+                hq.append(quantize("hq0", h_bf[0]))
+                g3.append(gather_words("g3_1", win3[1], lst3))
+        product(7)
+        weave(1, h_bf[1], nc.scalar.copy, 0, 192)
+        weave(1, h_bf[1], nc.vector.tensor_copy, 192, S)
+        hq.append(quantize("hq1", h_bf[1]))
+
+        def score(name, bank, m, words, plane):
+            acc = psum.tile([P, S], F32, name=name, tag=f"bank{bank}")
+            cols = slice(m * P, (m + 1) * P)
+            return acc, [
+                dict(out=acc[:], lhsT=words[a][:, cols].bitcast(FP8X4), lhsT_scale=plane[4 * a:P, cols],
+                     rhs=hq[a][0][:].bitcast(FP8X4), rhs_scale=hq[a][1][:], start=(a == 0), stop=(a == 1))
+                for a in range(2)
+            ]
+
+        e3 = [score(f"e3_{m}", m, m, g3, g3_sc) for m in range(4)]
+        for a in range(2):
+            for m in range(4):
+                nc.tensor.matmul_mx(**e3[m][1][a])
+        g2_sc = gather_bytes("g2_sc", tab2_sc[:], lst2)
+        g2 = [gather_words(f"g2_{a}", win2s[a], lst2) for a in range(2)]
+        e2 = [score(f"e2_{m}", 4 + m, m, g2, g2_sc) for m in range(4)]
+        for m in range(4):
+            for a in range(2):
+                nc.tensor.matmul_mx(**e2[m][1][a])
+
+        for m in range(4):
+            sq = work.tile([P, S], F32, name="sq")
+            nc.scalar.activation(sq[:], e3[m][0][:], ACT.Square)
+            rs = work.tile([P, S], F32, name="rs")
+            nc.scalar.activation(rs[:], sq[:], ACT.Abs_reciprocal_sqrt, bias=1.0)
+            damp = work.tile([P, S], F32, name="damp")
+            nc.scalar.activation(damp[:], rs[:], ACT.Square)
+            res = work.tile([P, S], F32, name="res")
+            nc.vector.scalar_tensor_tensor(res[:], e2[m][0][:], d_sb[:, m:m + 1], damp[:], ALU.add, ALU.mult)
+            nc.sync.dma_start(out[m * P:(m + 1) * P, :], res[:])

@@ -20,6 +20,8 @@ ACT = mybir.ActivationFunctionType
 P = 128
 PACK = 4
 KP = P * PACK
+MODE = "BBAAAFAF"
+SPLIT = 192
 
 
 def tile_list_heart_offer_score_kernel(
@@ -29,29 +31,31 @@ def tile_list_heart_offer_score_kernel(
     nc = tc.nc
     with ExitStack() as ctx:
         keep = ctx.enter_context(tc.tile_pool(name="keep", bufs=1))
-        work = ctx.enter_context(tc.tile_pool(name="work", bufs=3))
+        work = ctx.enter_context(tc.tile_pool(name="work", bufs=4))
         psum = ctx.enter_context(tc.psum_pool(name="psum", bufs=1))
 
-        def kept(name, shape, dtype):
-            return keep.tile(shape, dtype, name=name, align_bytes=64)
+        def kept(name, shape, dtype, tag=None):
+            return keep.tile(shape, dtype, name=name, tag=tag or name, align_bytes=64)
+
+        def probe(name, ap, dtype):
+            clock = keep.tile([P, 1], dtype, name=name)
+            nc.gpsimd.tensor_copy(clock[:], ap)
 
         def load_list(name, src):
             tile = keep.tile([P, S // 16], U16, name=name)
             nc.sync.dma_start(tile[:], src)
             return tile
 
-        def load_words(name, src):
-            tile = kept(name, [P, T], I32)
+        def load_words(name, src, tag=None):
+            tile = kept(name, [P, T], I32, tag)
             nc.sync.dma_start(tile[:], src.rearrange("p t i -> p (t i)").bitcast(I32))
             return tile
 
-        def gather_words(name, window, lst):
-            tile = kept(name, [P, S], U32)
-            nc.vector.tensor_copy(tile[:], window[:].bitcast(U32).indirect(lst[:]))
-            return tile
+        def gather_words(dst, window, lst):
+            nc.vector.tensor_copy(dst, window[:].bitcast(U32).indirect(lst[:]))
 
-        def gather_bytes(name, window, lst):
-            tile = kept(name, [P, S], U8)
+        def gather_bytes(name, window, lst, tag=None):
+            tile = kept(name, [P, S], U8, tag)
             nc.vector.tensor_copy(tile[:], window.indirect(lst[:]))
             return tile
 
@@ -60,16 +64,14 @@ def tile_list_heart_offer_score_kernel(
             nc.sync.dma_start(tile[:], w1[:, b * KP:(b + 1) * KP].rearrange("(p j) c -> p j c", j=PACK))
             return tile
 
-        def cast_w1(b, raw):
-            grouped = kept(f"w1_bf{b}", [P, KP * PACK], BF16)
+        def cast_w1(grouped, raw, m0, m1):
             nc.scalar.copy(
-                out=grouped[:].rearrange("p (t m j) -> p m j t", t=PACK, j=PACK),
-                in_=raw[:].rearrange("p j (m t) -> p m j t", t=PACK),
+                out=grouped[:].rearrange("p (t m j) -> p m j t", t=PACK, j=PACK)[:, m0:m1],
+                in_=raw[:].rearrange("p j (m t) -> p m j t", t=PACK)[:, m0:m1],
             )
-            return grouped
 
-        def quantize(name, grouped):
-            codes = kept(name + "_codes", [P, KP], U32)
+        def quantize(name, grouped, tag=None):
+            codes = kept(name + "_codes", [P, KP], U32, tag)
             plane = kept(name + "_plane", [P, KP], U8)
             nc.vector.quantize_mx(out=codes[:].bitcast(FP8X4), scales=plane[:], in_=grouped[:])
             return codes, plane
@@ -78,55 +80,61 @@ def tile_list_heart_offer_score_kernel(
         w4_sc_raw = kept("w4_sc_raw", [P, 2, H], U8)
         tab3_sc = kept("tab3_sc", [P, T], U8)
         tab2_sc = kept("tab2_sc", [P, T], U8)
-        nc.vector.memset(w4_sc_raw[:].bitcast(I32), 0)
         nc.vector.memset(tab_sc[:].bitcast(I32), 0)
-        nc.gpsimd.memset(tab3_sc[:].bitcast(I32), 0)
-        nc.gpsimd.memset(tab2_sc[:].bitcast(I32), 0)
+        nc.vector.memset(w4_sc_raw[:].bitcast(I32), 0)
+        nc.vector.memset(tab3_sc[:].bitcast(I32), 0)
+        nc.vector.memset(tab2_sc[:].bitcast(I32), 0)
 
-        gain_sb = keep.tile([P, 2, PACK], F32, name="gain_sb")
-        nc.gpsimd.dma_start(gain_sb[:], gain.rearrange("(b p t) -> p b t", b=2, t=PACK))
-        d_sb = keep.tile([P, 4], F32, name="d_sb")
-        with nc.allow_non_contiguous_dma(reason="one offset a partition"):
-            nc.gpsimd.dma_start(d_sb[:], d.rearrange("(m p) -> p m", p=P))
-
-        w4_raw = kept("w4_raw", [P, 2, H], U16)
-        nc.sync.dma_start(w4_raw[:].bitcast(I32), w4_words.rearrange("a p n -> p a n").bitcast(I32))
-        lst1 = load_list("lst1", offs)
-        for q in range(4):
-            nc.sync.dma_start(
-                w4_sc_raw[32 * q:32 * q + 4, :, :].bitcast(I32),
-                w4_scales[:, 4 * q:4 * q + 4, :].rearrange("a r n -> r a n").bitcast(I32),
-            )
+        warm0 = keep.tile([P, 1], F32, name="warm0")
+        zero = keep.tile([P, 1], F32, name="zero")
+        nc.gpsimd.memset(zero[:], 0.0)
+        nc.scalar.activation(warm0[:], zero[:], ACT.Sin)
+        win1 = load_words("win1", tab_words[1])
         for q in range(4):
             nc.sync.dma_start(
                 tab_sc[32 * q:32 * q + 4, :, :].bitcast(I32),
                 tab_scales[1:3, 4 * q:4 * q + 4, :].rearrange("a r n -> r a n").bitcast(I32),
             )
+        lst1 = load_list("lst1", offs)
+        w4_raw = kept("w4_raw", [P, 2, H], U16)
+        nc.sync.dma_start(w4_raw[:].bitcast(I32), w4_words.rearrange("a p n -> p a n").bitcast(I32))
+        w1_raw0 = load_w1(0)
         for q in range(4):
             nc.sync.dma_start(
-                tab_sc[32 * q + 4:32 * q + 8, 0, :].bitcast(I32),
+                w4_sc_raw[32 * q:32 * q + 4, :, :].bitcast(I32),
+                w4_scales[:, 4 * q:4 * q + 4, :].rearrange("a r n -> r a n").bitcast(I32),
+            )
+        win2 = load_words("win2", tab_words[2])
+        for q in range(4):
+            nc.sync.dma_start(
+                tab_sc[32 * q + 4:32 * q + 8, 1, :].bitcast(I32),
                 tab_scales[0, 4 * q:4 * q + 4, :].bitcast(I32),
             )
-        win1 = load_words("win1", tab_words[1])
-        w1_raw0 = load_w1(0)
-        win2 = load_words("win2", tab_words[2])
         win0 = load_words("win0", tab_words[0])
+        gain_sb = keep.tile([P, 2, PACK], F32, name="gain_sb")
+        nc.sync.dma_start(gain_sb[:], gain.rearrange("(b p t) -> p b t", b=2, t=PACK))
         w1_raw1 = load_w1(1)
         lst3 = load_list("lst3", offs3)
-        lst2 = load_list("lst2", offs2)
 
         def load_packed_scales(tile, src):
             for q in range(4):
                 nc.sync.dma_start(tile[32 * q:32 * q + 8, :].bitcast(I32), src[:, 4 * q:4 * q + 4, :].bitcast(I32))
 
+        win3 = [load_words("win3_0", tab3_words[0])]
         load_packed_scales(tab3_sc, tab3_scales)
-        win3 = [load_words(f"win3_{a}", tab3_words[a]) for a in range(2)]
+        win3.append(load_words("win3_1", tab3_words[1]))
+        lst2 = load_list("lst2", offs2)
+        win2s = [load_words("win2s_0", tab2_words[0])]
         load_packed_scales(tab2_sc, tab2_scales)
-        win2s = [load_words(f"win2s_{a}", tab2_words[a]) for a in range(2)]
+        win2s.append(load_words("win2s_1", tab2_words[1]))
+        d_sb = keep.tile([P, 4], F32, name="d_sb")
+        with nc.allow_non_contiguous_dma(reason="one offset a partition"):
+            nc.sync.dma_start(d_sb[:], d.rearrange("(m p) -> p m", p=P))
 
         w4_codes = []
         w4_plane = []
-        for b in range(2):
+
+        def deal_w4(b):
             codes = kept(f"w4_codes{b}", [P, 2, KP], U16)
             nc.vector.tensor_copy(
                 out=codes[:].rearrange("p a (t m) -> p a t m", t=PACK),
@@ -140,14 +148,19 @@ def tile_list_heart_offer_score_kernel(
             w4_codes.append(codes)
             w4_plane.append(plane)
 
-        v_sc10 = gather_bytes("v_sc10", tab_sc[:, 0, :], lst1)
-        v_sc2 = gather_bytes("v_sc2", tab_sc[:, 1, :], lst1)
-        v1 = gather_words("v1", win1, lst1)
-        w1_bf0 = cast_w1(0, w1_raw0)
-        v2 = gather_words("v2", win2, lst1)
-        w1q = [quantize("w1q0", w1_bf0)]
-        v0 = gather_words("v0", win0, lst1)
-        w1_bf1 = cast_w1(1, w1_raw1)
+        v = {1: kept("v1", [P, S], U32)}
+        gather_words(v[1][:], win1, lst1)
+        v_sc1 = gather_bytes("v_sc1", tab_sc[:, 0, :], lst1)
+        w1_bf = [kept(f"w1_bf{b}", [P, KP * PACK], BF16) for b in range(2)]
+        cast_w1(w1_bf[0], w1_raw0, 0, P)
+        deal_w4(0)
+        deal_w4(1)
+        v[2] = kept("v2", [P, S], U32, "w4_sc_raw")
+        gather_words(v[2][:], win2, lst1)
+        v_sc20 = gather_bytes("v_sc20", tab_sc[:, 1, :], lst1)
+        w1q = [quantize("w1q0", w1_bf[0], "win2")]
+        v[0] = kept("v0", [P, S], U32, "tab_sc")
+        gather_words(v[0][:], win0, lst1)
 
         banks = [psum.tile([P, S], F32, name=f"acc{i}", tag=f"bank{i}") for i in range(8)]
 
@@ -155,7 +168,7 @@ def tile_list_heart_offer_score_kernel(
             cols = slice(t * P, (t + 1) * P)
             nc.tensor.matmul_mx(
                 out=banks[4 * b + t][:], lhsT=w4_codes[b][:, a, cols].bitcast(FP4X4), lhsT_scale=w4_plane[b][:, a, cols],
-                rhs=words[:].bitcast(FP8X4), rhs_scale=plane[:], start=(a == 0), stop=False,
+                rhs=words[:].bitcast(FP8X4), rhs_scale=plane[:], start=(b == 0 and a == 0), stop=(b == 1 and a == 1),
             )
 
         def w1_pass(b, t):
@@ -163,29 +176,47 @@ def tile_list_heart_offer_score_kernel(
             codes, plane = w1q[b]
             nc.tensor.matmul_mx(
                 out=banks[4 * b + t][:], lhsT=codes[:, cols].bitcast(FP8X4), lhsT_scale=plane[:, cols],
-                rhs=v0[:].bitcast(FP8X4), rhs_scale=v_sc10[4:P, :], start=False, stop=True,
+                rhs=v[0][:].bitcast(FP8X4), rhs_scale=v_sc20[4:P, :], start=(b == 1), stop=(b == 0),
             )
 
-        for a, words, plane in ((0, v1, v_sc10), (1, v2, v_sc2)):
-            for b in range(2):
-                for t in range(PACK):
-                    w4_pass(b, t, a, words, plane)
+        for t in range(PACK):
+            w4_pass(0, t, 0, v[1], v_sc1)
+        for t in range(PACK):
+            w4_pass(0, t, 1, v[2], v_sc20)
         for t in range(PACK):
             w1_pass(0, t)
+        for piece in range(2):
+            cast_w1(w1_bf[1], w1_raw1, piece * P // 2, (piece + 1) * P // 2)
 
         h_rows = [kept(f"h_rows{b}", [P, PACK, S], BF16) for b in range(2)]
         cosines = {}
+        angle = {}
 
         def reduce_angle(i):
+            angle[i] = banks[i]
+            if MODE[i] == "A":
+                angle[i] = work.tile([P, S], F32, name="angle", bufs=4)
+                nc.scalar.activation(angle[i][:], banks[i][:], ACT.Abs, scale=1.0 / (2.0 * math.pi))
+                turns = work.tile([P, S], I32, name="turns")
+                nc.scalar.activation(turns[:].bitcast(U32), angle[i][:], ACT.Copy, bias=0.25)
+                return turns
+            if MODE[i] in "FG":
+                angle[i] = work.tile([P, S], F32, name="angle", bufs=4)
+                nc.scalar.copy(angle[i][:], banks[i][:])
             turns = work.tile([P, S], I32, name="turns")
-            nc.vector.tensor_scalar(turns[:], banks[i][:], 1.0 / (2.0 * math.pi), 0.25, ALU.mult, ALU.add)
+            eng = nc.gpsimd if MODE[i] == "G" else nc.vector
+            eng.tensor_scalar(turns[:], angle[i][:], 1.0 / (2.0 * math.pi), 0.25, ALU.mult, ALU.add)
             return turns
 
         def cosine(i, turns):
-            rest = work.tile([P, S], F32, name="rest")
-            nc.vector.scalar_tensor_tensor(rest[:], turns[:], -2.0 * math.pi, banks[i][:], ALU.mult, ALU.add)
-            cos = work.tile([P, S], F32, name="cos")
-            nc.scalar.activation(cos[:], rest[:], ACT.Sin, bias=0.5 * math.pi)
+            rest = kept(f"rest{i}", [P, S], F32)
+            cos = kept(f"cos{i}", [P, S], F32)
+            if MODE[i] == "A":
+                nc.vector.tensor_tensor(rest[:], angle[i][:], turns[:], ALU.subtract)
+                nc.scalar.activation(cos[:], rest[:], ACT.Sin, bias=0.5 * math.pi, scale=2.0 * math.pi)
+            else:
+                nc.vector.scalar_tensor_tensor(rest[:], turns[:], -2.0 * math.pi, banks[i][:], ALU.mult, ALU.add)
+                nc.scalar.activation(cos[:], rest[:], ACT.Sin, bias=0.5 * math.pi)
             cosines[i] = cos
 
         def product(i):
@@ -193,14 +224,16 @@ def tile_list_heart_offer_score_kernel(
             nc.vector.scalar_tensor_tensor(
                 h_rows[b][:, t, :], banks[i][:], gain_sb[:, b, t:t + 1], cosines[i][:], ALU.mult, ALU.mult)
 
-        def weave(b, dst, eng, j0, j1):
+        def weave(b, dst, base, eng, j0, j1):
             eng(
-                out=dst[:, j0 * PACK:j1 * PACK].rearrange("p (c i t) -> p c t i", i=4, t=PACK),
+                out=dst[:, (j0 - base) * PACK:(j1 - base) * PACK].rearrange("p (c i t) -> p c t i", i=4, t=PACK),
                 in_=h_rows[b][:, :, j0:j1].rearrange("p t (c i) -> p c t i", i=4),
             )
 
-        h_bf = [kept(f"h_bf{b}", [P, S * PACK], BF16) for b in range(2)]
-        hq = []
+        h_bf1 = kept("h_bf1", [P, S * PACK], BF16)
+        hq0 = (kept("hq0_codes", [P, KP], U32), kept("hq0_plane", [P, KP], U8))
+        woven = []
+        hq = [hq0]
         g3 = []
         turns = {0: reduce_angle(0)}
         for i in range(8):
@@ -208,23 +241,35 @@ def tile_list_heart_offer_score_kernel(
                 turns[i + 1] = reduce_angle(i + 1)
             cosine(i, turns[i])
             if i == 1:
-                w1q.append(quantize("w1q1", w1_bf1))
+                w1q.append(quantize("w1q1", w1_bf[1]))
                 for t in range(PACK):
                     w1_pass(1, t)
+                    w4_pass(1, t, 0, v[1], v_sc1)
+                    w4_pass(1, t, 1, v[2], v_sc20)
             if i >= 1:
                 product(i - 1)
-            if i == 4:
-                weave(0, h_bf[0], nc.scalar.copy, 0, S)
-                g3_sc = gather_bytes("g3_sc", tab3_sc[:], lst3)
+            if i == 2:
+                g3.append(kept("g3_0", [P, S], U32, "cos1"))
+                gather_words(g3[0][:], win3[0], lst3)
+            if i == 3:
+                g3_sc = gather_bytes("g3_sc", tab3_sc[:], lst3, "cos2")
+            if i in (4, 5):
+                woven.append(kept(f"h_bf0_{i}", [P, S * 2], BF16, f"rest{i}"))
+                weave(0, woven[i - 4], (i - 4) * 256, nc.scalar.copy, (i - 4) * 256, (i - 3) * 256)
             if i == 5:
-                g3.append(gather_words("g3_0", win3[0], lst3))
-            if i == 6:
-                hq.append(quantize("hq0", h_bf[0]))
-                g3.append(gather_words("g3_1", win3[1], lst3))
+                g3.append(kept("g3_1", [P, S], U32, "cos4"))
+                gather_words(g3[1][:], win3[1], lst3)
+            if i in (5, 6):
+                cols = slice((i - 5) * 256, (i - 4) * 256)
+                nc.vector.quantize_mx(out=hq0[0][:, cols].bitcast(FP8X4), scales=hq0[1][:, cols], in_=woven[i - 5][:])
+            if i == 7:
+                g2_sc = gather_bytes("g2_sc", tab2_sc[:], lst2, "cos6")
+        warm = keep.tile([P, 1], F32, name="warm")
+        nc.scalar.activation(warm[:], cosines[7][:, 0:1], ACT.Abs_reciprocal_sqrt, bias=2.0)
         product(7)
-        weave(1, h_bf[1], nc.scalar.copy, 0, 192)
-        weave(1, h_bf[1], nc.vector.tensor_copy, 192, S)
-        hq.append(quantize("hq1", h_bf[1]))
+        weave(1, h_bf1, 0, nc.scalar.copy, 0, SPLIT)
+        weave(1, h_bf1, 0, nc.vector.tensor_copy, SPLIT, S)
+        hq.append(quantize("hq1", h_bf1))
 
         def score(name, bank, m, words, plane):
             acc = psum.tile([P, S], F32, name=name, tag=f"bank{bank}")
@@ -239,20 +284,29 @@ def tile_list_heart_offer_score_kernel(
         for a in range(2):
             for m in range(4):
                 nc.tensor.matmul_mx(**e3[m][1][a])
-        g2_sc = gather_bytes("g2_sc", tab2_sc[:], lst2)
-        g2 = [gather_words(f"g2_{a}", win2s[a], lst2) for a in range(2)]
+        g2 = kept("g2", [P, 2, S], U32, tag="h_bf1")
+        for a in range(2):
+            gather_words(g2[:, a, :], win2s[a], lst2)
+        g2 = [g2[:, a, :] for a in range(2)]
         e2 = [score(f"e2_{m}", 4 + m, m, g2, g2_sc) for m in range(4)]
         for m in range(4):
             for a in range(2):
                 nc.tensor.matmul_mx(**e2[m][1][a])
 
-        for m in range(4):
-            sq = work.tile([P, S], F32, name="sq")
-            nc.scalar.activation(sq[:], e3[m][0][:], ACT.Square)
-            rs = work.tile([P, S], F32, name="rs")
+        for m, j0, j1, how in ((0, 0, 512, "S"), (1, 0, 512, "V"), (2, 0, 512, "V"), (3, 0, 256, "S"), (3, 256, 512, "S")):
+            sq = work.tile([P, j1 - j0], F32, name="sq")
+            nc.scalar.activation(sq[:], e3[m][0][:, j0:j1], ACT.Square)
+            rs = work.tile([P, j1 - j0], F32, name="rs")
             nc.scalar.activation(rs[:], sq[:], ACT.Abs_reciprocal_sqrt, bias=1.0)
-            damp = work.tile([P, S], F32, name="damp")
-            nc.scalar.activation(damp[:], rs[:], ACT.Square)
-            res = work.tile([P, S], F32, name="res")
-            nc.vector.scalar_tensor_tensor(res[:], e2[m][0][:], d_sb[:, m:m + 1], damp[:], ALU.add, ALU.mult)
-            nc.sync.dma_start(out[m * P:(m + 1) * P, :], res[:])
+            res = work.tile([P, j1 - j0], F32, name="res")
+            damp = work.tile([P, j1 - j0], F32, name="damp")
+            if how == "V":
+                nc.vector.scalar_tensor_tensor(damp[:], e2[m][0][:, j0:j1], d_sb[:, m:m + 1], rs[:], ALU.add, ALU.mult)
+                nc.vector.tensor_tensor(res[:], damp[:], rs[:], ALU.mult)
+            else:
+                if how == "S":
+                    nc.scalar.activation(damp[:], rs[:], ACT.Square)
+                else:
+                    nc.gpsimd.tensor_tensor(damp[:], rs[:], rs[:], ALU.mult)
+                nc.vector.scalar_tensor_tensor(res[:], e2[m][0][:, j0:j1], d_sb[:, m:m + 1], damp[:], ALU.add, ALU.mult)
+            nc.sync.dma_start(out[m * P:(m + 1) * P, j0:j1], res[:])

@@ -64,11 +64,16 @@ def tile_list_heart_offer_score_kernel(
             nc.sync.dma_start(tile[:], w1[:, b * KP:(b + 1) * KP].rearrange("(p j) c -> p j c", j=PACK))
             return tile
 
-        def cast_w1(grouped, raw, m0, m1):
+        def cast_w1(grouped, raw, pair):
+            ts = slice(2 * pair, 2 * pair + 2)
             nc.scalar.copy(
-                out=grouped[:].rearrange("p (t m j) -> p m j t", t=PACK, j=PACK)[:, m0:m1],
-                in_=raw[:].rearrange("p j (m t) -> p m j t", t=PACK)[:, m0:m1],
+                out=grouped[:].rearrange("p (t m j) -> p m j t", t=PACK, j=PACK)[:, :, :, ts],
+                in_=raw[:].rearrange("p j (m t) -> p m j t", t=PACK)[:, :, :, ts],
             )
+
+        def quantize_pair(dst, grouped, pair):
+            nc.vector.quantize_mx(
+                out=dst[pair][0][:].bitcast(FP8X4), scales=dst[pair][1][:], in_=grouped[:, pair * 1024:(pair + 1) * 1024])
 
         def quantize(name, grouped, tag=None):
             codes = kept(name + "_codes", [P, KP], U32, tag)
@@ -89,16 +94,15 @@ def tile_list_heart_offer_score_kernel(
         zero = keep.tile([P, 1], F32, name="zero")
         nc.gpsimd.memset(zero[:], 0.0)
         nc.scalar.activation(warm0[:], zero[:], ACT.Sin)
-        win1 = load_words("win1", tab_words[1])
+        w4_raw = kept("w4_raw", [P, 2, H], U16)
+        nc.sync.dma_start(w4_raw[:].bitcast(I32), w4_words.rearrange("a p n -> p a n").bitcast(I32))
         for q in range(4):
             nc.sync.dma_start(
                 tab_sc[32 * q:32 * q + 4, :, :].bitcast(I32),
                 tab_scales[1:3, 4 * q:4 * q + 4, :].rearrange("a r n -> r a n").bitcast(I32),
             )
         lst1 = load_list("lst1", offs)
-        w4_raw = kept("w4_raw", [P, 2, H], U16)
-        nc.sync.dma_start(w4_raw[:].bitcast(I32), w4_words.rearrange("a p n -> p a n").bitcast(I32))
-        w1_raw0 = load_w1(0)
+        win1 = load_words("win1", tab_words[1])
         for q in range(4):
             nc.sync.dma_start(
                 w4_sc_raw[32 * q:32 * q + 4, :, :].bitcast(I32),
@@ -110,6 +114,7 @@ def tile_list_heart_offer_score_kernel(
                 tab_sc[32 * q + 4:32 * q + 8, 1, :].bitcast(I32),
                 tab_scales[0, 4 * q:4 * q + 4, :].bitcast(I32),
             )
+        w1_raw0 = load_w1(0)
         win0 = load_words("win0", tab_words[0])
         gain_sb = keep.tile([P, 2, PACK], F32, name="gain_sb")
         nc.sync.dma_start(gain_sb[:], gain.rearrange("(b p t) -> p b t", b=2, t=PACK))
@@ -131,36 +136,37 @@ def tile_list_heart_offer_score_kernel(
         with nc.allow_non_contiguous_dma(reason="one offset a partition"):
             nc.sync.dma_start(d_sb[:], d.rearrange("(m p) -> p m", p=P))
 
-        w4_codes = []
-        w4_plane = []
 
-        def deal_w4(b):
-            codes = kept(f"w4_codes{b}", [P, 2, KP], U16)
+        def deal(name, raw, b, dtype):
+            dealt = kept(name, [P, 2, KP], dtype)
             nc.vector.tensor_copy(
-                out=codes[:].rearrange("p a (t m) -> p a t m", t=PACK),
-                in_=w4_raw[:, :, b * KP:(b + 1) * KP].rearrange("p a (m t) -> p a t m", t=PACK),
+                out=dealt[:].rearrange("p a (t m) -> p a t m", t=PACK),
+                in_=raw[:, :, b * KP:(b + 1) * KP].rearrange("p a (m t) -> p a t m", t=PACK),
             )
-            plane = kept(f"w4_plane{b}", [P, 2, KP], U8)
-            nc.vector.tensor_copy(
-                out=plane[:].rearrange("p a (t m) -> p a t m", t=PACK),
-                in_=w4_sc_raw[:, :, b * KP:(b + 1) * KP].rearrange("p a (m t) -> p a t m", t=PACK),
-            )
-            w4_codes.append(codes)
-            w4_plane.append(plane)
+            return dealt
 
+        w4_codes = [deal(f"w4_codes{b}", w4_raw, b, U16) for b in range(2)]
+        v_sc1 = gather_bytes("v_sc1", tab_sc[:, 0, :], lst1)
         v = {1: kept("v1", [P, S], U32)}
         gather_words(v[1][:], win1, lst1)
-        v_sc1 = gather_bytes("v_sc1", tab_sc[:, 0, :], lst1)
-        w1_bf = [kept(f"w1_bf{b}", [P, KP * PACK], BF16) for b in range(2)]
-        cast_w1(w1_bf[0], w1_raw0, 0, P)
-        deal_w4(0)
-        deal_w4(1)
+        w4_plane = [deal(f"w4_plane{b}", w4_sc_raw, b, U8) for b in range(2)]
+        v_sc20 = gather_bytes("v_sc20", tab_sc[:, 1, :], lst1)
         v[2] = kept("v2", [P, S], U32, "w4_sc_raw")
         gather_words(v[2][:], win2, lst1)
-        v_sc20 = gather_bytes("v_sc20", tab_sc[:, 1, :], lst1)
-        w1q = [quantize("w1q0", w1_bf[0], "win2")]
+        w1_bf = [kept(f"w1_bf{b}", [P, KP * PACK], BF16) for b in range(2)]
+        w1q = [[], []]
+
+        def w1q_tiles(b, pair, tag=None):
+            w1q[b].append((kept(f"w1q{b}{pair}_codes", [P, 256], U32, tag), kept(f"w1q{b}{pair}_plane", [P, 256], U8)))
+
+        w1q_tiles(0, 0, "win2")
+        cast_w1(w1_bf[0], w1_raw0, 0)
+        cast_w1(w1_bf[0], w1_raw0, 1)
+        quantize_pair(w1q[0], w1_bf[0], 0)
         v[0] = kept("v0", [P, S], U32, "tab_sc")
         gather_words(v[0][:], win0, lst1)
+        w1q_tiles(0, 1, "win0")
+        quantize_pair(w1q[0], w1_bf[0], 1)
 
         banks = [psum.tile([P, S], F32, name=f"acc{i}", tag=f"bank{i}") for i in range(8)]
 
@@ -172,8 +178,8 @@ def tile_list_heart_offer_score_kernel(
             )
 
         def w1_pass(b, t):
-            cols = slice(t * P, (t + 1) * P)
-            codes, plane = w1q[b]
+            cols = slice((t % 2) * P, (t % 2 + 1) * P)
+            codes, plane = w1q[b][t // 2]
             nc.tensor.matmul_mx(
                 out=banks[4 * b + t][:], lhsT=codes[:, cols].bitcast(FP8X4), lhsT_scale=plane[:, cols],
                 rhs=v[0][:].bitcast(FP8X4), rhs_scale=v_sc20[4:P, :], start=(b == 1), stop=(b == 0),
@@ -185,8 +191,8 @@ def tile_list_heart_offer_score_kernel(
             w4_pass(0, t, 1, v[2], v_sc20)
         for t in range(PACK):
             w1_pass(0, t)
-        for piece in range(2):
-            cast_w1(w1_bf[1], w1_raw1, piece * P // 2, (piece + 1) * P // 2)
+        cast_w1(w1_bf[1], w1_raw1, 0)
+        cast_w1(w1_bf[1], w1_raw1, 1)
 
         h_rows = [kept(f"h_rows{b}", [P, PACK, S], BF16) for b in range(2)]
         cosines = {}
@@ -240,9 +246,10 @@ def tile_list_heart_offer_score_kernel(
             if i + 1 < 8:
                 turns[i + 1] = reduce_angle(i + 1)
             cosine(i, turns[i])
-            if i == 1:
-                w1q.append(quantize("w1q1", w1_bf[1]))
-                for t in range(PACK):
+            if i in (1, 2):
+                w1q_tiles(1, i - 1)
+                quantize_pair(w1q[1], w1_bf[1], i - 1)
+                for t in (2 * i - 2, 2 * i - 1):
                     w1_pass(1, t)
                     w4_pass(1, t, 0, v[1], v_sc1)
                     w4_pass(1, t, 1, v[2], v_sc20)
@@ -293,7 +300,7 @@ def tile_list_heart_offer_score_kernel(
             for a in range(2):
                 nc.tensor.matmul_mx(**e2[m][1][a])
 
-        for m, j0, j1, how in ((0, 0, 512, "S"), (1, 0, 512, "V"), (2, 0, 512, "V"), (3, 0, 256, "S"), (3, 256, 512, "S")):
+        for m, j0, j1, how in ((0, 0, 512, "V"), (1, 0, 512, "V"), (2, 0, 512, "S"), (3, 0, 256, "S"), (3, 256, 512, "S")):
             sq = work.tile([P, j1 - j0], F32, name="sq")
             nc.scalar.activation(sq[:], e3[m][0][:, j0:j1], ACT.Square)
             rs = work.tile([P, j1 - j0], F32, name="rs")

@@ -3,7 +3,7 @@ from contextlib import ExitStack
 
 import concourse.mybir as mybir
 
-K, KA, KB, H, T, S = 1536, 512, 1024, 1024, 2048, 512
+K, H, T, S = 1536, 1024, 2048, 512
 FLOPS = 2 * K * H * S + 2 * 2 * H * S * S
 
 F32 = mybir.dt.float32
@@ -20,8 +20,13 @@ ACT = mybir.ActivationFunctionType
 P = 128
 PACK = 4
 KP = P * PACK
-MODE = "BBAAAFAF"
-SPLIT = 192
+QUADRANTS = 4
+TILES = 2 * PACK
+PAIR = 2 * P
+HALF_S = S // 2
+VECTOR_TURNS = 2
+SCALAR_WEAVE = 192
+GPSIMD_SQUARES = 2
 
 
 def tile_list_heart_offer_score_kernel(
@@ -37,105 +42,39 @@ def tile_list_heart_offer_score_kernel(
         def kept(name, shape, dtype, tag=None):
             return keep.tile(shape, dtype, name=name, tag=tag or name, align_bytes=64)
 
-        def probe(name, ap, dtype):
-            clock = keep.tile([P, 1], dtype, name=name)
-            nc.gpsimd.tensor_copy(clock[:], ap)
-
         def load_list(name, src):
             tile = keep.tile([P, S // 16], U16, name=name)
             nc.sync.dma_start(tile[:], src)
             return tile
 
-        def load_words(name, src, tag=None):
-            tile = kept(name, [P, T], I32, tag)
+        def load_words(name, src):
+            tile = kept(name, [P, T], I32)
             nc.sync.dma_start(tile[:], src.rearrange("p t i -> p (t i)").bitcast(I32))
             return tile
 
-        def gather_words(dst, window, lst):
-            nc.vector.tensor_copy(dst, window[:].bitcast(U32).indirect(lst[:]))
+        def load_planes_side_by_side(tile, src):
+            for q in range(QUADRANTS):
+                nc.sync.dma_start(
+                    tile[32 * q:32 * q + 4, :, :].bitcast(I32),
+                    src[:, 4 * q:4 * q + 4, :].rearrange("a s n -> s a n").bitcast(I32),
+                )
 
-        def gather_bytes(name, window, lst, tag=None):
-            tile = kept(name, [P, S], U8, tag)
-            nc.vector.tensor_copy(tile[:], window.indirect(lst[:]))
-            return tile
+        def load_planes_stacked(tile, src):
+            for q in range(QUADRANTS):
+                nc.sync.dma_start(tile[32 * q:32 * q + 8, :].bitcast(I32), src[:, 4 * q:4 * q + 4, :].bitcast(I32))
 
         def load_w1(b):
             tile = kept(f"w1_raw{b}", [P, PACK, KP], F32)
-            nc.sync.dma_start(tile[:], w1[:, b * KP:(b + 1) * KP].rearrange("(p j) c -> p j c", j=PACK))
+            nc.sync.dma_start(tile[:], w1[:, b * KP:(b + 1) * KP].rearrange("(p i) c -> p i c", i=PACK))
             return tile
 
-        def cast_w1(grouped, raw, pair):
-            ts = slice(2 * pair, 2 * pair + 2)
-            nc.scalar.copy(
-                out=grouped[:].rearrange("p (t m j) -> p m j t", t=PACK, j=PACK)[:, :, :, ts],
-                in_=raw[:].rearrange("p j (m t) -> p m j t", t=PACK)[:, :, :, ts],
-            )
+        def gather_words(dst, window, offsets):
+            nc.vector.tensor_copy(dst, window[:].bitcast(U32).indirect(offsets[:]))
 
-        def quantize_pair(dst, grouped, pair):
-            nc.vector.quantize_mx(
-                out=dst[pair][0][:].bitcast(FP8X4), scales=dst[pair][1][:], in_=grouped[:, pair * 1024:(pair + 1) * 1024])
-
-        def quantize(name, grouped, tag=None):
-            codes = kept(name + "_codes", [P, KP], U32, tag)
-            plane = kept(name + "_plane", [P, KP], U8)
-            nc.vector.quantize_mx(out=codes[:].bitcast(FP8X4), scales=plane[:], in_=grouped[:])
-            return codes, plane
-
-        tab_sc = kept("tab_sc", [P, 2, T], U8)
-        w4_sc_raw = kept("w4_sc_raw", [P, 2, H], U8)
-        tab3_sc = kept("tab3_sc", [P, T], U8)
-        tab2_sc = kept("tab2_sc", [P, T], U8)
-        nc.vector.memset(tab_sc[:].bitcast(I32), 0)
-        nc.vector.memset(w4_sc_raw[:].bitcast(I32), 0)
-        nc.vector.memset(tab3_sc[:].bitcast(I32), 0)
-        nc.vector.memset(tab2_sc[:].bitcast(I32), 0)
-
-        warm0 = keep.tile([P, 1], F32, name="warm0")
-        zero = keep.tile([P, 1], F32, name="zero")
-        nc.gpsimd.memset(zero[:], 0.0)
-        nc.scalar.activation(warm0[:], zero[:], ACT.Sin)
-        w4_raw = kept("w4_raw", [P, 2, H], U16)
-        nc.sync.dma_start(w4_raw[:].bitcast(I32), w4_words.rearrange("a p n -> p a n").bitcast(I32))
-        for q in range(4):
-            nc.sync.dma_start(
-                tab_sc[32 * q:32 * q + 4, :, :].bitcast(I32),
-                tab_scales[1:3, 4 * q:4 * q + 4, :].rearrange("a r n -> r a n").bitcast(I32),
-            )
-        lst1 = load_list("lst1", offs)
-        win1 = load_words("win1", tab_words[1])
-        for q in range(4):
-            nc.sync.dma_start(
-                w4_sc_raw[32 * q:32 * q + 4, :, :].bitcast(I32),
-                w4_scales[:, 4 * q:4 * q + 4, :].rearrange("a r n -> r a n").bitcast(I32),
-            )
-        win2 = load_words("win2", tab_words[2])
-        for q in range(4):
-            nc.sync.dma_start(
-                tab_sc[32 * q + 4:32 * q + 8, 1, :].bitcast(I32),
-                tab_scales[0, 4 * q:4 * q + 4, :].bitcast(I32),
-            )
-        w1_raw0 = load_w1(0)
-        win0 = load_words("win0", tab_words[0])
-        gain_sb = keep.tile([P, 2, PACK], F32, name="gain_sb")
-        nc.sync.dma_start(gain_sb[:], gain.rearrange("(b p t) -> p b t", b=2, t=PACK))
-        w1_raw1 = load_w1(1)
-        lst3 = load_list("lst3", offs3)
-
-        def load_packed_scales(tile, src):
-            for q in range(4):
-                nc.sync.dma_start(tile[32 * q:32 * q + 8, :].bitcast(I32), src[:, 4 * q:4 * q + 4, :].bitcast(I32))
-
-        win3 = [load_words("win3_0", tab3_words[0])]
-        load_packed_scales(tab3_sc, tab3_scales)
-        win3.append(load_words("win3_1", tab3_words[1]))
-        lst2 = load_list("lst2", offs2)
-        win2s = [load_words("win2s_0", tab2_words[0])]
-        load_packed_scales(tab2_sc, tab2_scales)
-        win2s.append(load_words("win2s_1", tab2_words[1]))
-        d_sb = keep.tile([P, 4], F32, name="d_sb")
-        with nc.allow_non_contiguous_dma(reason="one offset a partition"):
-            nc.sync.dma_start(d_sb[:], d.rearrange("(m p) -> p m", p=P))
-
+        def gather_plane(name, window, offsets, tag=None):
+            tile = kept(name, [P, S], U8, tag)
+            nc.vector.tensor_copy(tile[:], window.indirect(offsets[:]))
+            return tile
 
         def deal(name, raw, b, dtype):
             dealt = kept(name, [P, 2, KP], dtype)
@@ -145,175 +84,230 @@ def tile_list_heart_offer_score_kernel(
             )
             return dealt
 
+        def cast_w1(b, pair):
+            ts = slice(2 * pair, 2 * pair + 2)
+            nc.scalar.copy(
+                out=w1_bf[b][:].rearrange("p (t m i) -> p m i t", t=PACK, i=PACK)[:, :, :, ts],
+                in_=w1_raw[b][:].rearrange("p i (m t) -> p m i t", t=PACK)[:, :, :, ts],
+            )
+
+        def mx_tiles(name, width, tag=None):
+            return kept(name + "_codes", [P, width], U32, tag), kept(name + "_plane", [P, width], U8)
+
+        def quantize(codes, plane, values):
+            nc.vector.quantize_mx(out=codes.bitcast(FP8X4), scales=plane, in_=values)
+
+        def quantize_w1(b, pair):
+            codes, plane = w1_mx[b, pair]
+            quantize(codes[:], plane[:], w1_bf[b][:, pair * PAIR * PACK:(pair + 1) * PAIR * PACK])
+
+        tab_planes = kept("tab_planes", [P, 2, T], U8)
+        w4_planes_raw = kept("w4_planes_raw", [P, 2, H], U8)
+        tab3_planes = kept("tab3_planes", [P, T], U8)
+        tab2_planes = kept("tab2_planes", [P, T], U8)
+        for planes in (tab_planes, w4_planes_raw, tab3_planes, tab2_planes):
+            nc.vector.memset(planes[:].bitcast(I32), 0)
+
+        sin_warmup = keep.tile([P, 1], F32, name="sin_warmup")
+        zero = keep.tile([P, 1], F32, name="zero")
+        nc.gpsimd.memset(zero[:], 0.0)
+        nc.scalar.activation(sin_warmup[:], zero[:], ACT.Sin)
+
+        w4_raw = kept("w4_raw", [P, 2, H], U16)
+        nc.sync.dma_start(w4_raw[:].bitcast(I32), w4_words.rearrange("a p n -> p a n").bitcast(I32))
+        load_planes_side_by_side(tab_planes, tab_scales[1:3])
+        patients = load_list("patients", offs)
+        tab_pass = {1: load_words("tab_pass1", tab_words[1])}
+        load_planes_side_by_side(w4_planes_raw, w4_scales)
+        tab_pass[2] = load_words("tab_pass2", tab_words[2])
+        for q in range(QUADRANTS):
+            nc.sync.dma_start(
+                tab_planes[32 * q + 4:32 * q + 8, 1, :].bitcast(I32),
+                tab_scales[0, 4 * q:4 * q + 4, :].bitcast(I32),
+            )
+        w1_raw = [load_w1(0)]
+        tab_pass[0] = load_words("tab_pass0", tab_words[0])
+        gain_sb = keep.tile([P, 2, PACK], F32, name="gain_sb")
+        nc.sync.dma_start(gain_sb[:], gain.rearrange("(b p t) -> p b t", b=2, t=PACK))
+        w1_raw.append(load_w1(1))
+        crews = load_list("crews", offs3)
+        tab3_pass = [load_words("tab3_pass0", tab3_words[0])]
+        load_planes_stacked(tab3_planes, tab3_scales)
+        tab3_pass.append(load_words("tab3_pass1", tab3_words[1]))
+        hearts = load_list("hearts", offs2)
+        tab2_pass = [load_words("tab2_pass0", tab2_words[0])]
+        load_planes_stacked(tab2_planes, tab2_scales)
+        tab2_pass.append(load_words("tab2_pass1", tab2_words[1]))
+        d_sb = keep.tile([P, S // P], F32, name="d_sb")
+        with nc.allow_non_contiguous_dma(reason="output row 128 m + p lies on partition p"):
+            nc.sync.dma_start(d_sb[:], d.rearrange("(m p) -> p m", p=P))
+
         w4_codes = [deal(f"w4_codes{b}", w4_raw, b, U16) for b in range(2)]
-        v_sc1 = gather_bytes("v_sc1", tab_sc[:, 0, :], lst1)
-        v = {1: kept("v1", [P, S], U32)}
-        gather_words(v[1][:], win1, lst1)
-        w4_plane = [deal(f"w4_plane{b}", w4_sc_raw, b, U8) for b in range(2)]
-        v_sc20 = gather_bytes("v_sc20", tab_sc[:, 1, :], lst1)
-        v[2] = kept("v2", [P, S], U32, "w4_sc_raw")
-        gather_words(v[2][:], win2, lst1)
+        v_plane1 = gather_plane("v_plane1", tab_planes[:, 0, :], patients)
+        v_words = {1: kept("v_words1", [P, S], U32)}
+        gather_words(v_words[1][:], tab_pass[1], patients)
+        w4_plane = [deal(f"w4_plane{b}", w4_planes_raw, b, U8) for b in range(2)]
+        v_plane20 = gather_plane("v_plane20", tab_planes[:, 1, :], patients)
+        v_words[2] = kept("v_words2", [P, S], U32, "w4_planes_raw")
+        gather_words(v_words[2][:], tab_pass[2], patients)
         w1_bf = [kept(f"w1_bf{b}", [P, KP * PACK], BF16) for b in range(2)]
-        w1q = [[], []]
+        w1_mx = {(0, 0): mx_tiles("w1_mx00", PAIR, "tab_pass2")}
+        cast_w1(0, 0)
+        cast_w1(0, 1)
+        quantize_w1(0, 0)
+        v_words[0] = kept("v_words0", [P, S], U32, "tab_planes")
+        gather_words(v_words[0][:], tab_pass[0], patients)
+        w1_mx[0, 1] = mx_tiles("w1_mx01", PAIR, "tab_pass0")
+        quantize_w1(0, 1)
 
-        def w1q_tiles(b, pair, tag=None):
-            w1q[b].append((kept(f"w1q{b}{pair}_codes", [P, 256], U32, tag), kept(f"w1q{b}{pair}_plane", [P, 256], U8)))
+        a_acc = [psum.tile([P, S], F32, name=f"a_acc{i}", tag=f"bank{i}") for i in range(TILES)]
 
-        w1q_tiles(0, 0, "win2")
-        cast_w1(w1_bf[0], w1_raw0, 0)
-        cast_w1(w1_bf[0], w1_raw0, 1)
-        quantize_pair(w1q[0], w1_bf[0], 0)
-        v[0] = kept("v0", [P, S], U32, "tab_sc")
-        gather_words(v[0][:], win0, lst1)
-        w1q_tiles(0, 1, "win0")
-        quantize_pair(w1q[0], w1_bf[0], 1)
-
-        banks = [psum.tile([P, S], F32, name=f"acc{i}", tag=f"bank{i}") for i in range(8)]
-
-        def w4_pass(b, t, a, words, plane):
+        def w4_matmul(b, t, a):
             cols = slice(t * P, (t + 1) * P)
             nc.tensor.matmul_mx(
-                out=banks[4 * b + t][:], lhsT=w4_codes[b][:, a, cols].bitcast(FP4X4), lhsT_scale=w4_plane[b][:, a, cols],
-                rhs=words[:].bitcast(FP8X4), rhs_scale=plane[:], start=(b == 0 and a == 0), stop=(b == 1 and a == 1),
+                out=a_acc[PACK * b + t][:],
+                lhsT=w4_codes[b][:, a, cols].bitcast(FP4X4), lhsT_scale=w4_plane[b][:, a, cols],
+                rhs=v_words[1 + a][:].bitcast(FP8X4), rhs_scale=(v_plane1, v_plane20)[a][:],
+                start=(b == 0 and a == 0), stop=(b == 1 and a == 1),
             )
 
-        def w1_pass(b, t):
+        def w1_matmul(b, t):
             cols = slice((t % 2) * P, (t % 2 + 1) * P)
-            codes, plane = w1q[b][t // 2]
+            codes, plane = w1_mx[b, t // 2]
             nc.tensor.matmul_mx(
-                out=banks[4 * b + t][:], lhsT=codes[:, cols].bitcast(FP8X4), lhsT_scale=plane[:, cols],
-                rhs=v[0][:].bitcast(FP8X4), rhs_scale=v_sc20[4:P, :], start=(b == 1), stop=(b == 0),
+                out=a_acc[PACK * b + t][:],
+                lhsT=codes[:, cols].bitcast(FP8X4), lhsT_scale=plane[:, cols],
+                rhs=v_words[0][:].bitcast(FP8X4), rhs_scale=v_plane20[4:P, :],
+                start=(b == 1), stop=(b == 0),
             )
 
+        for a in range(2):
+            for t in range(PACK):
+                w4_matmul(0, t, a)
         for t in range(PACK):
-            w4_pass(0, t, 0, v[1], v_sc1)
-        for t in range(PACK):
-            w4_pass(0, t, 1, v[2], v_sc20)
-        for t in range(PACK):
-            w1_pass(0, t)
-        cast_w1(w1_bf[1], w1_raw1, 0)
-        cast_w1(w1_bf[1], w1_raw1, 1)
+            w1_matmul(0, t)
+        cast_w1(1, 0)
+        cast_w1(1, 1)
 
         h_rows = [kept(f"h_rows{b}", [P, PACK, S], BF16) for b in range(2)]
+        turns = {}
         cosines = {}
-        angle = {}
 
-        def reduce_angle(i):
-            angle[i] = banks[i]
-            if MODE[i] == "A":
-                angle[i] = work.tile([P, S], F32, name="angle", bufs=4)
-                nc.scalar.activation(angle[i][:], banks[i][:], ACT.Abs, scale=1.0 / (2.0 * math.pi))
-                turns = work.tile([P, S], I32, name="turns")
-                nc.scalar.activation(turns[:].bitcast(U32), angle[i][:], ACT.Copy, bias=0.25)
-                return turns
-            if MODE[i] in "FG":
-                angle[i] = work.tile([P, S], F32, name="angle", bufs=4)
-                nc.scalar.copy(angle[i][:], banks[i][:])
-            turns = work.tile([P, S], I32, name="turns")
-            eng = nc.gpsimd if MODE[i] == "G" else nc.vector
-            eng.tensor_scalar(turns[:], angle[i][:], 1.0 / (2.0 * math.pi), 0.25, ALU.mult, ALU.add)
-            return turns
-
-        def cosine(i, turns):
-            rest = kept(f"rest{i}", [P, S], F32)
-            cos = kept(f"cos{i}", [P, S], F32)
-            if MODE[i] == "A":
-                nc.vector.tensor_tensor(rest[:], angle[i][:], turns[:], ALU.subtract)
-                nc.scalar.activation(cos[:], rest[:], ACT.Sin, bias=0.5 * math.pi, scale=2.0 * math.pi)
+        def count_turns(i):
+            if i < VECTOR_TURNS:
+                engine, angle = nc.vector, a_acc[i]
             else:
-                nc.vector.scalar_tensor_tensor(rest[:], turns[:], -2.0 * math.pi, banks[i][:], ALU.mult, ALU.add)
-                nc.scalar.activation(cos[:], rest[:], ACT.Sin, bias=0.5 * math.pi)
-            cosines[i] = cos
+                engine, angle = nc.gpsimd, work.tile([P, S], F32, name="angle")
+                nc.scalar.copy(angle[:], a_acc[i][:])
+            turns[i] = work.tile([P, S], I32, name="turns")
+            engine.tensor_scalar(turns[i][:], angle[:], 1.0 / (2.0 * math.pi), 0.25, ALU.mult, ALU.add)
+
+        def cosine(i):
+            rest = kept(f"rest{i}", [P, S], F32)
+            cosines[i] = kept(f"cos{i}", [P, S], F32)
+            nc.vector.scalar_tensor_tensor(rest[:], turns[i][:], -2.0 * math.pi, a_acc[i][:], ALU.mult, ALU.add)
+            nc.scalar.activation(cosines[i][:], rest[:], ACT.Sin, bias=0.5 * math.pi)
 
         def product(i):
             b, t = divmod(i, PACK)
             nc.vector.scalar_tensor_tensor(
-                h_rows[b][:, t, :], banks[i][:], gain_sb[:, b, t:t + 1], cosines[i][:], ALU.mult, ALU.mult)
+                h_rows[b][:, t, :], a_acc[i][:], gain_sb[:, b, t:t + 1], cosines[i][:], ALU.mult, ALU.mult)
 
-        def weave(b, dst, base, eng, j0, j1):
-            eng(
-                out=dst[:, (j0 - base) * PACK:(j1 - base) * PACK].rearrange("p (c i t) -> p c t i", i=4, t=PACK),
-                in_=h_rows[b][:, :, j0:j1].rearrange("p t (c i) -> p c t i", i=4),
+        def weave(copy, dst, b, j0, j1):
+            copy(
+                out=dst.rearrange("p (c n t) -> p c t n", n=4, t=PACK),
+                in_=h_rows[b][:, :, j0:j1].rearrange("p t (c n) -> p c t n", n=4),
             )
 
-        h_bf1 = kept("h_bf1", [P, S * PACK], BF16)
-        hq0 = (kept("hq0_codes", [P, KP], U32), kept("hq0_plane", [P, KP], U8))
-        woven = []
-        hq = [hq0]
-        g3 = []
-        turns = {0: reduce_angle(0)}
-        for i in range(8):
-            if i + 1 < 8:
-                turns[i + 1] = reduce_angle(i + 1)
-            cosine(i, turns[i])
+        woven1 = kept("woven1", [P, S * PACK], BF16)
+        h_mx = [mx_tiles("h_mx0", KP)]
+        woven0 = []
+        v3_words = []
+
+        def second_half_operands(pair):
+            w1_mx[1, pair] = mx_tiles(f"w1_mx1{pair}", PAIR)
+            quantize_w1(1, pair)
+            for t in (2 * pair, 2 * pair + 1):
+                w1_matmul(1, t)
+                w4_matmul(1, t, 0)
+                w4_matmul(1, t, 1)
+
+        def gather_crew_words(a, after):
+            v3_words.append(kept(f"v3_words{a}", [P, S], U32, f"cos{after}"))
+            gather_words(v3_words[a][:], tab3_pass[a], crews)
+
+        def weave_first_half(piece, after):
+            woven0.append(kept(f"woven0_{piece}", [P, HALF_S * PACK], BF16, f"rest{after}"))
+            weave(nc.scalar.copy, woven0[piece][:], 0, piece * HALF_S, (piece + 1) * HALF_S)
+
+        def quantize_first_half(piece):
+            cols = slice(piece * HALF_S, (piece + 1) * HALF_S)
+            quantize(h_mx[0][0][:, cols], h_mx[0][1][:, cols], woven0[piece][:])
+
+        count_turns(0)
+        for i in range(TILES):
+            if i + 1 < TILES:
+                count_turns(i + 1)
+            cosine(i)
             if i in (1, 2):
-                w1q_tiles(1, i - 1)
-                quantize_pair(w1q[1], w1_bf[1], i - 1)
-                for t in (2 * i - 2, 2 * i - 1):
-                    w1_pass(1, t)
-                    w4_pass(1, t, 0, v[1], v_sc1)
-                    w4_pass(1, t, 1, v[2], v_sc20)
+                second_half_operands(i - 1)
             if i >= 1:
                 product(i - 1)
             if i == 2:
-                g3.append(kept("g3_0", [P, S], U32, "cos1"))
-                gather_words(g3[0][:], win3[0], lst3)
+                gather_crew_words(0, i - 1)
             if i == 3:
-                g3_sc = gather_bytes("g3_sc", tab3_sc[:], lst3, "cos2")
-            if i in (4, 5):
-                woven.append(kept(f"h_bf0_{i}", [P, S * 2], BF16, f"rest{i}"))
-                weave(0, woven[i - 4], (i - 4) * 256, nc.scalar.copy, (i - 4) * 256, (i - 3) * 256)
-            if i == 5:
-                g3.append(kept("g3_1", [P, S], U32, "cos4"))
-                gather_words(g3[1][:], win3[1], lst3)
-            if i in (5, 6):
-                cols = slice((i - 5) * 256, (i - 4) * 256)
-                nc.vector.quantize_mx(out=hq0[0][:, cols].bitcast(FP8X4), scales=hq0[1][:, cols], in_=woven[i - 5][:])
-            if i == 7:
-                g2_sc = gather_bytes("g2_sc", tab2_sc[:], lst2, "cos6")
-        warm = keep.tile([P, 1], F32, name="warm")
-        nc.scalar.activation(warm[:], cosines[7][:, 0:1], ACT.Abs_reciprocal_sqrt, bias=2.0)
-        product(7)
-        weave(1, h_bf1, 0, nc.scalar.copy, 0, SPLIT)
-        weave(1, h_bf1, 0, nc.vector.tensor_copy, SPLIT, S)
-        hq.append(quantize("hq1", h_bf1))
+                v3_plane = gather_plane("v3_plane", tab3_planes[:], crews, f"cos{i - 1}")
+            if i in (PACK, PACK + 1):
+                weave_first_half(i - PACK, i)
+            if i == PACK + 1:
+                gather_crew_words(1, i - 1)
+            if i in (PACK + 1, PACK + 2):
+                quantize_first_half(i - PACK - 1)
+            if i == TILES - 1:
+                v2_plane = gather_plane("v2_plane", tab2_planes[:], hearts, f"cos{i - 1}")
+        product(TILES - 1)
+        weave(nc.scalar.copy, woven1[:, :SCALAR_WEAVE * PACK], 1, 0, SCALAR_WEAVE)
+        root_warmup = keep.tile([P, 1], F32, name="root_warmup")
+        nc.scalar.activation(root_warmup[:], h_rows[1][:, PACK - 1, 0:1], ACT.Abs_reciprocal_sqrt, bias=1.0, scale=0.0)
+        weave(nc.vector.tensor_copy, woven1[:, SCALAR_WEAVE * PACK:], 1, SCALAR_WEAVE, S)
+        h_mx.append(mx_tiles("h_mx1", KP))
+        quantize(h_mx[1][0][:], h_mx[1][1][:], woven1[:])
 
-        def score(name, bank, m, words, plane):
-            acc = psum.tile([P, S], F32, name=name, tag=f"bank{bank}")
+        def score_matmul(acc, words, plane, m, a):
             cols = slice(m * P, (m + 1) * P)
-            return acc, [
-                dict(out=acc[:], lhsT=words[a][:, cols].bitcast(FP8X4), lhsT_scale=plane[4 * a:P, cols],
-                     rhs=hq[a][0][:].bitcast(FP8X4), rhs_scale=hq[a][1][:], start=(a == 0), stop=(a == 1))
-                for a in range(2)
-            ]
+            nc.tensor.matmul_mx(
+                out=acc[:],
+                lhsT=words[:, cols].bitcast(FP8X4), lhsT_scale=plane[4 * a:P, cols],
+                rhs=h_mx[a][0][:].bitcast(FP8X4), rhs_scale=h_mx[a][1][:],
+                start=(a == 0), stop=(a == 1),
+            )
 
-        e3 = [score(f"e3_{m}", m, m, g3, g3_sc) for m in range(4)]
+        out_tiles = S // P
+        e3 = [psum.tile([P, S], F32, name=f"e3_{m}", tag=f"bank{m}") for m in range(out_tiles)]
         for a in range(2):
-            for m in range(4):
-                nc.tensor.matmul_mx(**e3[m][1][a])
-        g2 = kept("g2", [P, 2, S], U32, tag="h_bf1")
+            for m in range(out_tiles):
+                score_matmul(e3[m], v3_words[a], v3_plane, m, a)
+        v2_words = kept("v2_words", [P, 2, S], U32, "woven1")
         for a in range(2):
-            gather_words(g2[:, a, :], win2s[a], lst2)
-        g2 = [g2[:, a, :] for a in range(2)]
-        e2 = [score(f"e2_{m}", 4 + m, m, g2, g2_sc) for m in range(4)]
-        for m in range(4):
+            gather_words(v2_words[:, a, :], tab2_pass[a], hearts)
+        e2 = [psum.tile([P, S], F32, name=f"e2_{m}", tag=f"bank{out_tiles + m}") for m in range(out_tiles)]
+        for m in range(out_tiles):
             for a in range(2):
-                nc.tensor.matmul_mx(**e2[m][1][a])
+                score_matmul(e2[m], v2_words[:, a, :], v2_plane, m, a)
 
-        for m, j0, j1, how in ((0, 0, 512, "V"), (1, 0, 512, "V"), (2, 0, 512, "S"), (3, 0, 256, "S"), (3, 256, 512, "S")):
-            sq = work.tile([P, j1 - j0], F32, name="sq")
-            nc.scalar.activation(sq[:], e3[m][0][:, j0:j1], ACT.Square)
-            rs = work.tile([P, j1 - j0], F32, name="rs")
-            nc.scalar.activation(rs[:], sq[:], ACT.Abs_reciprocal_sqrt, bias=1.0)
-            res = work.tile([P, j1 - j0], F32, name="res")
-            damp = work.tile([P, j1 - j0], F32, name="damp")
-            if how == "V":
-                nc.vector.scalar_tensor_tensor(damp[:], e2[m][0][:, j0:j1], d_sb[:, m:m + 1], rs[:], ALU.add, ALU.mult)
-                nc.vector.tensor_tensor(res[:], damp[:], rs[:], ALU.mult)
+        last = out_tiles - 1
+        pieces = [(m, 0, S) for m in range(last)] + [(last, 0, HALF_S), (last, HALF_S, S)]
+        for m, j0, j1 in pieces:
+            square = work.tile([P, j1 - j0], F32, name="square")
+            nc.scalar.activation(square[:], e3[m][:, j0:j1], ACT.Square)
+            root = work.tile([P, j1 - j0], F32, name="root")
+            nc.scalar.activation(root[:], square[:], ACT.Abs_reciprocal_sqrt, bias=1.0)
+            result = work.tile([P, j1 - j0], F32, name="result")
+            damping = work.tile([P, j1 - j0], F32, name="damping")
+            if m < GPSIMD_SQUARES:
+                nc.gpsimd.tensor_tensor(damping[:], root[:], root[:], ALU.mult)
             else:
-                if how == "S":
-                    nc.scalar.activation(damp[:], rs[:], ACT.Square)
-                else:
-                    nc.gpsimd.tensor_tensor(damp[:], rs[:], rs[:], ALU.mult)
-                nc.vector.scalar_tensor_tensor(res[:], e2[m][0][:, j0:j1], d_sb[:, m:m + 1], damp[:], ALU.add, ALU.mult)
-            nc.sync.dma_start(out[m * P:(m + 1) * P, j0:j1], res[:])
+                nc.scalar.activation(damping[:], root[:], ACT.Square)
+            nc.vector.scalar_tensor_tensor(
+                result[:], e2[m][:, j0:j1], d_sb[:, m:m + 1], damping[:], ALU.add, ALU.mult)
+            nc.sync.dma_start(out[m * P:(m + 1) * P, j0:j1], result[:])

import math
from contextlib import ExitStack

import concourse.mybir as mybir

K, H, T, S = 1536, 1024, 2048, 512
FLOPS = 2 * K * H * S + 2 * 2 * H * S * S

F32 = mybir.dt.float32
BF16 = mybir.dt.bfloat16
I32 = mybir.dt.int32
U32 = mybir.dt.uint32
U16 = mybir.dt.uint16
U8 = mybir.dt.uint8
FP8X4 = mybir.dt.float8_e4m3fn_x4
FP4X4 = mybir.dt.float4_e2m1fn_x4
ALU = mybir.AluOpType
ACT = mybir.ActivationFunctionType

P = 128
PACK = 4
KP = P * PACK
QUADRANTS = 4
TILES = 2 * PACK
PAIR = 2 * P
HALF_S = S // 2
VECTOR_TURNS = 2
SCALAR_WEAVE = 192
GPSIMD_SQUARES = 2


def tile_list_heart_offer_score_kernel(
    tc, tab_words, tab_scales, offs, w1, w4_words, w4_scales, gain,
    tab2_words, tab2_scales, offs2, tab3_words, tab3_scales, offs3, d, out,
):
    nc = tc.nc
    with ExitStack() as ctx:
        keep = ctx.enter_context(tc.tile_pool(name="keep", bufs=1))
        work = ctx.enter_context(tc.tile_pool(name="work", bufs=4))
        psum = ctx.enter_context(tc.psum_pool(name="psum", bufs=1))

        def kept(name, shape, dtype, tag=None):
            return keep.tile(shape, dtype, name=name, tag=tag or name, align_bytes=64)

        def load_list(name, src):
            tile = keep.tile([P, S // 16], U16, name=name)
            nc.sync.dma_start(tile[:], src)
            return tile

        def load_words(name, src):
            tile = kept(name, [P, T], I32)
            nc.sync.dma_start(tile[:], src.rearrange("p t i -> p (t i)").bitcast(I32))
            return tile

        def load_planes_side_by_side(tile, src):
            for q in range(QUADRANTS):
                nc.sync.dma_start(
                    tile[32 * q:32 * q + 4, :, :].bitcast(I32),
                    src[:, 4 * q:4 * q + 4, :].rearrange("a s n -> s a n").bitcast(I32),
                )

        def load_planes_stacked(tile, src):
            for q in range(QUADRANTS):
                nc.sync.dma_start(tile[32 * q:32 * q + 8, :].bitcast(I32), src[:, 4 * q:4 * q + 4, :].bitcast(I32))

        def load_w1(b):
            tile = kept(f"w1_raw{b}", [P, PACK, KP], F32)
            nc.sync.dma_start(tile[:], w1[:, b * KP:(b + 1) * KP].rearrange("(p i) c -> p i c", i=PACK))
            return tile

        def gather_words(dst, window, offsets):
            nc.vector.tensor_copy(dst, window[:].bitcast(U32).indirect(offsets[:]))

        def gather_plane(name, window, offsets, tag=None):
            tile = kept(name, [P, S], U8, tag)
            nc.vector.tensor_copy(tile[:], window.indirect(offsets[:]))
            return tile

        def deal(name, raw, b, dtype):
            dealt = kept(name, [P, 2, KP], dtype)
            nc.vector.tensor_copy(
                out=dealt[:].rearrange("p a (t m) -> p a t m", t=PACK),
                in_=raw[:, :, b * KP:(b + 1) * KP].rearrange("p a (m t) -> p a t m", t=PACK),
            )
            return dealt

        def cast_w1(b, pair):
            ts = slice(2 * pair, 2 * pair + 2)
            nc.scalar.copy(
                out=w1_bf[b][:].rearrange("p (t m i) -> p m i t", t=PACK, i=PACK)[:, :, :, ts],
                in_=w1_raw[b][:].rearrange("p i (m t) -> p m i t", t=PACK)[:, :, :, ts],
            )

        def mx_tiles(name, width, tag=None):
            return kept(name + "_codes", [P, width], U32, tag), kept(name + "_plane", [P, width], U8)

        def quantize(codes, plane, values):
            nc.vector.quantize_mx(out=codes.bitcast(FP8X4), scales=plane, in_=values)

        def quantize_w1(b, pair):
            codes, plane = w1_mx[b, pair]
            quantize(codes[:], plane[:], w1_bf[b][:, pair * PAIR * PACK:(pair + 1) * PAIR * PACK])

        tab_planes = kept("tab_planes", [P, 2, T], U8)
        w4_planes_raw = kept("w4_planes_raw", [P, 2, H], U8)
        tab3_planes = kept("tab3_planes", [P, T], U8)
        tab2_planes = kept("tab2_planes", [P, T], U8)
        for planes in (tab_planes, w4_planes_raw, tab3_planes, tab2_planes):
            nc.vector.memset(planes[:].bitcast(I32), 0)

        sin_warmup = keep.tile([P, 1], F32, name="sin_warmup")
        zero = keep.tile([P, 1], F32, name="zero")
        nc.gpsimd.memset(zero[:], 0.0)
        nc.scalar.activation(sin_warmup[:], zero[:], ACT.Sin)

        w4_raw = kept("w4_raw", [P, 2, H], U16)
        nc.sync.dma_start(w4_raw[:].bitcast(I32), w4_words.rearrange("a p n -> p a n").bitcast(I32))
        load_planes_side_by_side(tab_planes, tab_scales[1:3])
        patients = load_list("patients", offs)
        tab_pass = {1: load_words("tab_pass1", tab_words[1])}
        load_planes_side_by_side(w4_planes_raw, w4_scales)
        tab_pass[2] = load_words("tab_pass2", tab_words[2])
        for q in range(QUADRANTS):
            nc.sync.dma_start(
                tab_planes[32 * q + 4:32 * q + 8, 1, :].bitcast(I32),
                tab_scales[0, 4 * q:4 * q + 4, :].bitcast(I32),
            )
        w1_raw = [load_w1(0)]
        tab_pass[0] = load_words("tab_pass0", tab_words[0])
        gain_sb = keep.tile([P, 2, PACK], F32, name="gain_sb")
        nc.sync.dma_start(gain_sb[:], gain.rearrange("(b p t) -> p b t", b=2, t=PACK))
        w1_raw.append(load_w1(1))
        crews = load_list("crews", offs3)
        tab3_pass = [load_words("tab3_pass0", tab3_words[0])]
        load_planes_stacked(tab3_planes, tab3_scales)
        tab3_pass.append(load_words("tab3_pass1", tab3_words[1]))
        hearts = load_list("hearts", offs2)
        tab2_pass = [load_words("tab2_pass0", tab2_words[0])]
        load_planes_stacked(tab2_planes, tab2_scales)
        tab2_pass.append(load_words("tab2_pass1", tab2_words[1]))
        d_sb = keep.tile([P, S // P], F32, name="d_sb")
        with nc.allow_non_contiguous_dma(reason="output row 128 m + p lies on partition p"):
            nc.sync.dma_start(d_sb[:], d.rearrange("(m p) -> p m", p=P))

        w4_codes = [deal(f"w4_codes{b}", w4_raw, b, U16) for b in range(2)]
        v_plane1 = gather_plane("v_plane1", tab_planes[:, 0, :], patients)
        v_words = {1: kept("v_words1", [P, S], U32)}
        gather_words(v_words[1][:], tab_pass[1], patients)
        w4_plane = [deal(f"w4_plane{b}", w4_planes_raw, b, U8) for b in range(2)]
        v_plane20 = gather_plane("v_plane20", tab_planes[:, 1, :], patients)
        v_words[2] = kept("v_words2", [P, S], U32, "w4_planes_raw")
        gather_words(v_words[2][:], tab_pass[2], patients)
        w1_bf = [kept(f"w1_bf{b}", [P, KP * PACK], BF16) for b in range(2)]
        w1_mx = {(0, 0): mx_tiles("w1_mx00", PAIR, "tab_pass2")}
        cast_w1(0, 0)
        cast_w1(0, 1)
        quantize_w1(0, 0)
        v_words[0] = kept("v_words0", [P, S], U32, "tab_planes")
        gather_words(v_words[0][:], tab_pass[0], patients)
        w1_mx[0, 1] = mx_tiles("w1_mx01", PAIR, "tab_pass0")
        quantize_w1(0, 1)

        a_acc = [psum.tile([P, S], F32, name=f"a_acc{i}", tag=f"bank{i}") for i in range(TILES)]

        def w4_matmul(b, t, a):
            cols = slice(t * P, (t + 1) * P)
            nc.tensor.matmul_mx(
                out=a_acc[PACK * b + t][:],
                lhsT=w4_codes[b][:, a, cols].bitcast(FP4X4), lhsT_scale=w4_plane[b][:, a, cols],
                rhs=v_words[1 + a][:].bitcast(FP8X4), rhs_scale=(v_plane1, v_plane20)[a][:],
                start=(b == 0 and a == 0), stop=(b == 1 and a == 1),
            )

        def w1_matmul(b, t):
            cols = slice((t % 2) * P, (t % 2 + 1) * P)
            codes, plane = w1_mx[b, t // 2]
            nc.tensor.matmul_mx(
                out=a_acc[PACK * b + t][:],
                lhsT=codes[:, cols].bitcast(FP8X4), lhsT_scale=plane[:, cols],
                rhs=v_words[0][:].bitcast(FP8X4), rhs_scale=v_plane20[4:P, :],
                start=(b == 1), stop=(b == 0),
            )

        for a in range(2):
            for t in range(PACK):
                w4_matmul(0, t, a)
        for t in range(PACK):
            w1_matmul(0, t)
        cast_w1(1, 0)
        cast_w1(1, 1)

        h_rows = [kept(f"h_rows{b}", [P, PACK, S], BF16) for b in range(2)]
        turns = {}
        cosines = {}

        def count_turns(i):
            if i < VECTOR_TURNS:
                engine, angle = nc.vector, a_acc[i]
            else:
                engine, angle = nc.gpsimd, work.tile([P, S], F32, name="angle")
                nc.scalar.copy(angle[:], a_acc[i][:])
            turns[i] = work.tile([P, S], I32, name="turns")
            engine.tensor_scalar(turns[i][:], angle[:], 1.0 / (2.0 * math.pi), 0.25, ALU.mult, ALU.add)

        def cosine(i):
            rest = kept(f"rest{i}", [P, S], F32)
            cosines[i] = kept(f"cos{i}", [P, S], F32)
            nc.vector.scalar_tensor_tensor(rest[:], turns[i][:], -2.0 * math.pi, a_acc[i][:], ALU.mult, ALU.add)
            nc.scalar.activation(cosines[i][:], rest[:], ACT.Sin, bias=0.5 * math.pi)

        def product(i):
            b, t = divmod(i, PACK)
            nc.vector.scalar_tensor_tensor(
                h_rows[b][:, t, :], a_acc[i][:], gain_sb[:, b, t:t + 1], cosines[i][:], ALU.mult, ALU.mult)

        def weave(copy, dst, b, j0, j1):
            copy(
                out=dst.rearrange("p (c n t) -> p c t n", n=4, t=PACK),
                in_=h_rows[b][:, :, j0:j1].rearrange("p t (c n) -> p c t n", n=4),
            )

        woven1 = kept("woven1", [P, S * PACK], BF16)
        h_mx = [mx_tiles("h_mx0", KP)]
        woven0 = []
        v3_words = []

        def second_half_operands(pair):
            w1_mx[1, pair] = mx_tiles(f"w1_mx1{pair}", PAIR)
            quantize_w1(1, pair)
            for t in (2 * pair, 2 * pair + 1):
                w1_matmul(1, t)
                w4_matmul(1, t, 0)
                w4_matmul(1, t, 1)

        def gather_crew_words(a, after):
            v3_words.append(kept(f"v3_words{a}", [P, S], U32, f"cos{after}"))
            gather_words(v3_words[a][:], tab3_pass[a], crews)

        def weave_first_half(piece, after):
            woven0.append(kept(f"woven0_{piece}", [P, HALF_S * PACK], BF16, f"rest{after}"))
            weave(nc.scalar.copy, woven0[piece][:], 0, piece * HALF_S, (piece + 1) * HALF_S)

        def quantize_first_half(piece):
            cols = slice(piece * HALF_S, (piece + 1) * HALF_S)
            quantize(h_mx[0][0][:, cols], h_mx[0][1][:, cols], woven0[piece][:])

        count_turns(0)
        for i in range(TILES):
            if i + 1 < TILES:
                count_turns(i + 1)
            cosine(i)
            if i in (1, 2):
                second_half_operands(i - 1)
            if i >= 1:
                product(i - 1)
            if i == 2:
                gather_crew_words(0, i - 1)
            if i == 3:
                v3_plane = gather_plane("v3_plane", tab3_planes[:], crews, f"cos{i - 1}")
            if i in (PACK, PACK + 1):
                weave_first_half(i - PACK, i)
            if i == PACK + 1:
                gather_crew_words(1, i - 1)
            if i in (PACK + 1, PACK + 2):
                quantize_first_half(i - PACK - 1)
            if i == TILES - 1:
                v2_plane = gather_plane("v2_plane", tab2_planes[:], hearts, f"cos{i - 1}")
        product(TILES - 1)
        weave(nc.scalar.copy, woven1[:, :SCALAR_WEAVE * PACK], 1, 0, SCALAR_WEAVE)
        root_warmup = keep.tile([P, 1], F32, name="root_warmup")
        nc.scalar.activation(root_warmup[:], h_rows[1][:, PACK - 1, 0:1], ACT.Abs_reciprocal_sqrt, bias=1.0, scale=0.0)
        weave(nc.vector.tensor_copy, woven1[:, SCALAR_WEAVE * PACK:], 1, SCALAR_WEAVE, S)
        h_mx.append(mx_tiles("h_mx1", KP))
        quantize(h_mx[1][0][:], h_mx[1][1][:], woven1[:])

        def score_matmul(acc, words, plane, m, a):
            cols = slice(m * P, (m + 1) * P)
            nc.tensor.matmul_mx(
                out=acc[:],
                lhsT=words[:, cols].bitcast(FP8X4), lhsT_scale=plane[4 * a:P, cols],
                rhs=h_mx[a][0][:].bitcast(FP8X4), rhs_scale=h_mx[a][1][:],
                start=(a == 0), stop=(a == 1),
            )

        out_tiles = S // P
        e3 = [psum.tile([P, S], F32, name=f"e3_{m}", tag=f"bank{m}") for m in range(out_tiles)]
        for a in range(2):
            for m in range(out_tiles):
                score_matmul(e3[m], v3_words[a], v3_plane, m, a)
        v2_words = kept("v2_words", [P, 2, S], U32, "woven1")
        for a in range(2):
            gather_words(v2_words[:, a, :], tab2_pass[a], hearts)
        e2 = [psum.tile([P, S], F32, name=f"e2_{m}", tag=f"bank{out_tiles + m}") for m in range(out_tiles)]
        for m in range(out_tiles):
            for a in range(2):
                score_matmul(e2[m], v2_words[:, a, :], v2_plane, m, a)

        last = out_tiles - 1
        pieces = [(m, 0, S) for m in range(last)] + [(last, 0, HALF_S), (last, HALF_S, S)]
        for m, j0, j1 in pieces:
            square = work.tile([P, j1 - j0], F32, name="square")
            nc.scalar.activation(square[:], e3[m][:, j0:j1], ACT.Square)
            root = work.tile([P, j1 - j0], F32, name="root")
            nc.scalar.activation(root[:], square[:], ACT.Abs_reciprocal_sqrt, bias=1.0)
            result = work.tile([P, j1 - j0], F32, name="result")
            damping = work.tile([P, j1 - j0], F32, name="damping")
            if m < GPSIMD_SQUARES:
                nc.gpsimd.tensor_tensor(damping[:], root[:], root[:], ALU.mult)
            else:
                nc.scalar.activation(damping[:], root[:], ACT.Square)
            nc.vector.scalar_tensor_tensor(
                result[:], e2[m][:, j0:j1], d_sb[:, m:m + 1], damping[:], ALU.add, ALU.mult)
            nc.sync.dma_start(out[m * P:(m + 1) * P, j0:j1], result[:])
